import numpy as np
import ml_dtypes


def mxq(x, axis, fmt="e4m3"):
    dtype, down = {"e4m3": (ml_dtypes.float8_e4m3fn, 7), "e5m2": (ml_dtypes.float8_e5m2, 14)}[fmt]
    v = np.moveaxis(np.asarray(x, np.float32).astype(ml_dtypes.bfloat16).astype(np.float64), axis, -1)
    blocks = v.reshape(v.shape[:-1] + (-1, 32))
    amax = np.abs(blocks).max(-1, keepdims=True)
    byte = np.maximum(np.where(amax > 0, np.frexp(amax)[1] - 1 + 127, 0) - down, 1)
    scale = np.exp2(byte - 127.0)
    codes = (blocks / scale).astype(np.float32).astype(dtype).astype(np.float64)
    return np.moveaxis((codes * scale).reshape(v.shape), -1, axis)


WIDE = False


def mx_kscale(k):
    if not WIDE:
        return np.ones(k)
    levels = np.array([10, -10, 5, -5, 0])
    if k % 512:
        return np.exp2(np.random.permutation(np.resize(levels, k // 32))).repeat(32)
    a = np.empty((k // 512, 16))
    for p in range(k // 512):
        a[p, :8] = np.random.permutation(np.resize(levels, 8))
        for g in range(8):
            far = levels[np.abs(levels - a[p, g]) >= 10]
            a[p, g + 8] = far[np.random.randint(len(far))]
    return np.exp2(a.ravel()).repeat(32)


def f64(x):
    return np.asarray(x).astype(np.float64)


def striped(idx):
    return np.tile(np.asarray(idx).reshape(-1, 16).T, (8, 1)).astype(np.uint16)


def unstriped(offs):
    return offs[:16].T.reshape(-1).astype(np.int64)


E2M1 = np.array([0.0, 0.5, 1.0, 1.5, 2.0, 3.0, 4.0, 6.0, -0.0, -0.5, -1.0, -1.5, -2.0, -3.0, -4.0, -6.0])


def pack_weight(w, fmt):
    k, n = w.shape
    w = f64(np.asarray(w, np.float32).astype(ml_dtypes.bfloat16)).reshape(k // 32, 32, n)
    amax = np.abs(w).max(1)
    if fmt == "e4m3":
        byte = np.frexp(amax)[1] - 1 + 127 - 7
    else:
        mant, ex = np.frexp(amax / 6.0)
        byte = np.where(mant > 0.5, ex, ex - 1) + 127
    byte = np.clip(np.where(amax > 0, byte, 1), 1, 254)
    scaled = (w * np.exp2(127.0 - byte)[:, None, :]).reshape(k, n).astype(np.float32)
    by_word = np.ascontiguousarray(scaled.reshape(k // 512, 128, 4, n).transpose(0, 1, 3, 2))
    if fmt == "e4m3":
        words = by_word.astype(ml_dtypes.float8_e4m3fn).view(np.uint8)
    else:
        c = by_word.astype(ml_dtypes.float4_e2m1fn).view(np.uint8) & 0xF
        words = (c[..., 0::2] | (c[..., 1::2] << 4)).reshape(k // 512, 128, 2 * n)
    return np.ascontiguousarray(words), np.ascontiguousarray(byte.astype(np.uint8).reshape(k // 512, 16, n))


def unpack_weight(words, scales, fmt):
    g, _, n = scales.shape
    words = np.ascontiguousarray(words).reshape(g, 128, n, -1)
    if fmt == "e4m3":
        vals = words.view(ml_dtypes.float8_e4m3fn).astype(np.float64)
    else:
        nib = np.empty((g, 128, n, 4), np.uint8)
        nib[..., 0::2] = words & 0xF
        nib[..., 1::2] = words >> 4
        vals = E2M1[nib]
    vals = vals * np.repeat(np.exp2(scales.astype(np.float64) - 127.0), 8, axis=1)[..., None]
    return vals.transpose(0, 1, 3, 2).reshape(g * 512, n)


def bf(x):
    return np.asarray(x, np.float32).astype(ml_dtypes.bfloat16)


def planes(Y):
    r, m = Y.shape
    b = f64(bf(Y)).reshape(r // 32, 32, m)
    amax = np.abs(b).max(1)
    byte = np.clip(np.where(amax > 0, np.frexp(amax)[1] - 1 + 127 - 7, 1), 1, 254)
    codes = (b * np.exp2(127.0 - byte)[:, None, :]).reshape(r, m).astype(np.float32).astype(ml_dtypes.float8_e4m3fn).view(np.uint8)
    words = codes.reshape(r // 512, 128, 4, m).transpose(0, 1, 3, 2)
    return np.ascontiguousarray(words), np.ascontiguousarray(byte.astype(np.uint8).reshape(r // 512, 16, m))


D, T, I, Q, E, H = 512, 2048, 512, 256, 512, 32


def setup_inputs():
    n = np.random.standard_normal
    idx = np.random.permutation(T)[:I]
    fd = mx_kscale(D)
    fi = mx_kscale(I)
    keysp = pack_weight(n((D, T)) / fd[:, None], "e2m1")
    return {
        "query": (n((D, Q)) * 0.65 / np.sqrt(D) * fd[:, None]).astype(np.float32),
        "keys_words": keysp[0],
        "keys_scales": keysp[1],
        "lowend": np.tile(np.random.uniform(-1.5, 0.0, T), (128, 1)).astype(np.float32),
        "highend": np.tile(np.random.uniform(0.0, 1.5, T), (128, 1)).astype(np.float32),
        "lam": (np.random.uniform(0.8, 2.0, (Q, 1))).astype(np.float32),
        "averse": (np.random.uniform(0.4, 1.0, (Q, 1))).astype(np.float32),
        "os": (np.random.uniform(4.0, 16.0, (1, I)) * fi).astype(np.float32),
        "vals": (n((E, T))).astype(np.float32),
        "vsc": (np.random.uniform(0.5, 2.0, (1, I)) / fi).astype(np.float32),
        "offs": striped(idx),
    }


def reference(query, keys_words, keys_scales, lowend, highend, lam, averse, os, vals, vsc, offs):
    idx = unstriped(offs)
    keysu = unpack_weight(keys_words, keys_scales, "e2m1")
    queryq = mxq(f64(query), 0, "e4m3")
    keysidxg = keysu[:, idx]
    a = queryq.T @ keysidxg
    s = np.minimum(a - f64(lowend)[:1][:, idx], f64(highend)[:1][:, idx] - a) * f64(lam)
    p = np.exp(s - np.max(s, axis=1, keepdims=True))
    r = p / np.sum(p, axis=1, keepdims=True)
    p2 = np.exp(s * (-1.0) - np.max(s * (-1.0), axis=1, keepdims=True))
    r2 = p2 / np.sum(p2, axis=1, keepdims=True)
    w = r - r2 * f64(averse)
    wo1 = w * f64(os)
    wt1 = wo1.T
    vg = f64(vals)[:, idx].reshape(E, H, I // H).mean(axis=2)
    vgr = np.repeat(vg, I // H, axis=1)
    vd = (f64(vals)[:, idx] - vgr) * f64(vsc)
    vt1 = vd.T
    vt1q = mxq(vt1, 0, "e4m3")
    wt1q = mxq(wt1, 0, "e4m3")
    o = vt1q.T @ wt1q
    words, scales = planes(o)
    return o, words, scales

@@ -1,0 +1,242 @@
+from contextlib import ExitStack
+
+import concourse.mybir as mybir
+from concourse.masks import make_identity
+
+D, T, I, Q, E = 512, 2048, 512, 256, 512
+STRETCH = 16
+P = 128
+PACK = 4
+
+FLOPS = 2 * D * Q * I + 2 * I * E * Q
+BYTES = 4 * D * Q + D * T // 2 + D * T // 32 + 2 * 4 * T + 2 * 4 * Q + 2 * 4 * I + 4 * E * T + 2 * P * I // 16 + 5 * E * Q + E * Q // 32
+
+F32 = mybir.dt.float32
+BF16 = mybir.dt.bfloat16
+I32 = mybir.dt.int32
+U32 = mybir.dt.uint32
+U16 = mybir.dt.uint16
+U8 = mybir.dt.uint8
+FP8X4 = mybir.dt.float8_e4m3fn_x4
+FP4X4 = mybir.dt.float4_e2m1fn_x4
+ALU = mybir.AluOpType
+ACT = mybir.ActivationFunctionType
+AXIS = mybir.AxisListType
+
+
+def tile_attend_interval_twoside_centredvalues_pl_kernel(
+    tc, query, keys_words, keys_scales, lowend, highend, lam, averse, wfac, vals, vsc, offs, out_0, out_1, out_2
+):
+    nc = tc.nc
+    with ExitStack() as ctx:
+        sb = ctx.enter_context(tc.tile_pool(name="sb", bufs=1))
+        ps = ctx.enter_context(tc.psum_pool(name="ps", bufs=1))
+
+        def bank(tag, shape, name):
+            return ps.tile(shape, F32, name=name, tag=tag)
+
+        offsets = sb.tile([P, I // 16], U16, name="offsets")
+        nc.sync.dma_start(offsets[:], offs)
+        kw = sb.tile([P, T], U16, name="kw")
+        nc.sync.dma_start(kw[:].bitcast(I32), keys_words[0].bitcast(I32))
+        ks = sb.tile([P, T], U8, name="ks")
+        for quad in range(4):
+            rows = keys_scales[0, 4 * quad : 4 * quad + 4, :].bitcast(I32)
+            nc.sync.dma_start(ks[32 * quad : 32 * (quad + 1), :].bitcast(I32), rows.unsqueeze(0).to_broadcast([8, 4, T // 4]))
+        hi_win = sb.tile([P, T], F32, name="hi_win")
+        lo_win = sb.tile([P, T], F32, name="lo_win")
+        for win, src in ((hi_win, highend), (lo_win, lowend)):
+            nc.vector.memset(win[0 : P - 1, :], 0.0)
+            nc.sync.dma_start(win[P - 1 : P, :], src[0:1, :])
+        q_raw = sb.tile([P, PACK, Q], F32, name="q_raw")
+        nc.sync.dma_start(q_raw[:], query.rearrange("(p j) q -> p j q", j=PACK))
+        vals_rows = vals.rearrange("(p j) t -> p j t", j=PACK)
+        v_win = [sb.tile([P, T], F32, name=f"v_win{j}", tag=f"v_win{j}") for j in range(PACK)]
+        lam_t = sb.tile([P, 2], F32, name="lam_t")
+        avr_t = sb.tile([P, 2], F32, name="avr_t")
+        vsc_t = sb.tile([P, PACK], F32, name="vsc_t")
+        wfac_t = sb.tile([P, PACK], F32, name="wfac_t")
+        nc.sync.dma_start(v_win[0][:], vals_rows[:, 0, :])
+        with nc.allow_non_contiguous_dma(reason="one value a partition"):
+            nc.sync.dma_start(lam_t[:], lam.rearrange("(c p) o -> p (c o)", p=P))
+        nc.sync.dma_start(vsc_t[:], vsc.rearrange("o (p t) -> p (o t)", t=PACK))
+        nc.sync.dma_start(v_win[1][:], vals_rows[:, 1, :])
+        with nc.allow_non_contiguous_dma(reason="one value a partition"):
+            nc.sync.dma_start(avr_t[:], averse.rearrange("(c p) o -> p (c o)", p=P))
+        nc.sync.dma_start(wfac_t[:], wfac.rearrange("o (p t) -> p (o t)", t=PACK))
+        nc.sync.dma_start(v_win[2][:], vals_rows[:, 2, :])
+        nc.sync.dma_start(v_win[3][:], vals_rows[:, 3, :])
+
+        ident_bf = sb.tile([P, P], BF16, name="ident_bf")
+        make_identity(nc, ident_bf[:])
+        ident = sb.tile([P, P], F32, name="ident")
+        nc.scalar.activation(ident[:], ident_bf[:], ACT.Copy)
+
+        kg = [sb.tile([P, I // 2], U16, name=f"kg{h}", align_bytes=64) for h in range(2)]
+        ksg = [sb.tile([P, I // 2], U8, name=f"ksg{h}", align_bytes=64) for h in range(2)]
+        q_il = sb.tile([P, Q, PACK], BF16, name="q_il", align_bytes=64)
+        q_codes = sb.tile([P, Q], U32, name="q_codes", align_bytes=64)
+        q_scales = sb.tile([P, Q], U8, name="q_scales", align_bytes=64)
+
+        def gather_keys(h):
+            half = offsets[:, 16 * h : 16 * (h + 1)]
+            nc.vector.tensor_copy(kg[h][:], kw[:].indirect(half))
+            nc.vector.tensor_copy(ksg[h][:], ks[:].indirect(half))
+
+        hi_picked = sb.tile([P, I], F32, name="hi_picked")
+        lo_picked = sb.tile([P, I], F32, name="lo_picked")
+        nc.scalar.activation(hi_picked[:], hi_win[:].indirect(offsets[:]), ACT.Copy)
+        gather_keys(0)
+        nc.vector.tensor_copy(lo_picked[:], lo_win[:].indirect(offsets[:]))
+        nc.scalar.copy(
+            q_il[:].rearrange("p (c i) j -> p c j i", i=4), q_raw[:].rearrange("p j (c i) -> p c j i", i=4)
+        )
+        gather_keys(1)
+        nc.vector.quantize_mx(q_codes[:].bitcast(FP8X4), q_scales[:], q_il[:].rearrange("p q j -> p (q j)"))
+
+        ends = []
+        for picked, tag in ((hi_picked, "c2"), (lo_picked, "c3")):
+            turned = bank(tag, [P, 4, P], f"turned_{tag}")
+            for c in range(4):
+                nc.tensor.transpose(turned[:, c, :], picked[:, c * P : (c + 1) * P], ident[:])
+            col = sb.tile([P, 4], F32, name=f"col_{tag}", tag=f"col_{tag}")
+            nc.scalar.copy(col[:], turned[:, :, P - 1])
+            ends.append(col)
+        hi_col, lo_col = ends
+
+        margin = []
+        for c, tag in enumerate(("a0", "a1", "c0", "c1")):
+            a = bank(tag, [P, Q], f"a{c}")
+            cols = slice((c % 2) * P, (c % 2 + 1) * P)
+            nc.tensor.matmul_mx(
+                a[:], lhsT=kg[c // 2][:, cols].bitcast(FP4X4), lhsT_scale=ksg[c // 2][:, cols],
+                rhs=q_codes[:].bitcast(FP8X4), rhs_scale=q_scales[:], start=True, stop=True,
+            )
+            up = sb.tile([P, Q], F32, name=f"up{c}")
+            nc.scalar.activation(up[:], a[:], ACT.Identity, bias=hi_col[:, c : c + 1], scale=-1.0)
+            m = sb.tile([P, Q], F32, name=f"m{c}")
+            nc.vector.scalar_tensor_tensor(m[:], a[:], lo_col[:, c : c + 1], up[:], ALU.subtract, ALU.min)
+            margin.append(m)
+
+        m_ps = [bank(f"b{h}", [P, I], f"m_ps{h}") for h in range(2)]
+        for h in range(2):
+            for c in range(4):
+                nc.tensor.transpose(m_ps[h][:, c * P : (c + 1) * P], margin[c][:, h * P : (h + 1) * P], ident[:])
+
+        navr = sb.tile([P, 2], F32, name="navr")
+        nc.gpsimd.tensor_scalar(navr[:], avr_t[:], -1.0, 0.0, ALU.mult, ALU.add)
+
+        s = [sb.tile([P, PACK, P], F32, name=f"s{h}") for h in range(2)]
+        smin = [sb.tile([P, 1], F32, name=f"smin{h}") for h in range(2)]
+        nsmax = [sb.tile([P, 1], F32, name=f"nsmax{h}") for h in range(2)]
+        for h in range(2):
+            nc.vector.tensor_scalar(
+                s[h][:], m_ps[h][:].rearrange("q (s t) -> q t s", t=PACK), lam_t[:, h : h + 1], None, ALU.mult, ALU.min,
+                accum_out=smin[h][:],
+            )
+        for h in range(2):
+            nc.vector.tensor_reduce(nsmax[h][:], s[h][:].rearrange("q t s -> q (t s)"), AXIS.X, ALU.max, negate=True)
+
+        def values(j):
+            g = sb.tile([P, I], F32, name=f"g{j}", tag=("col_c2" if j == 0 else f"g{j}"))
+            if j < PACK - 1:
+                nc.scalar.activation(g[:], v_win[j][:].indirect(offsets[:]), ACT.Copy)
+            else:
+                nc.scalar.activation(g[:, 0 : I // 2], v_win[j][:].indirect(offsets[:, 0:16]), ACT.Copy)
+                nc.vector.tensor_copy(g[:, I // 2 : I], v_win[j][:].indirect(offsets[:, 16:32]))
+            if j < PACK - 1:
+                part = g[:].rearrange("e (h u) -> e h u", u=STRETCH)
+                width = STRETCH
+                while width > 1:
+                    width = width // 2
+                    halved = sb.tile([P, I // STRETCH, width], F32, name=f"vpart{j}_{width}")
+                    nc.gpsimd.tensor_tensor(halved[:], part[:, :, 0:width], part[:, :, width : 2 * width], ALU.add)
+                    part = halved[:]
+                total = part
+            else:
+                sums = sb.tile([P, I // STRETCH], F32, name=f"vsum{j}")
+                nc.vector.tensor_reduce(sums[:], g[:].rearrange("e (h u) -> e h u", u=STRETCH), AXIS.X, ALU.add)
+                total = sums[:].unsqueeze(2)
+            nmean = sb.tile([P, I // STRETCH, 4], F32, name=f"nmean{j}")
+            nc.gpsimd.tensor_scalar(
+                nmean[:], total.to_broadcast([P, I // STRETCH, 4]), -1.0 / STRETCH, 0.0, ALU.mult, ALU.add
+            )
+            vt = bank(f"c{j}", [P, PACK, P], f"vt{j}")
+            for t in range(PACK):
+                nc.tensor.matmul(vt[:, t, :], lhsT=g[:, t::PACK], rhs=ident[:], is_transpose=True, start=(t == 0), stop=False)
+            for t in range(PACK):
+                nc.tensor.matmul(
+                    vt[:, t, :], lhsT=nmean[:].rearrange("e h r -> e (h r)"), rhs=ident[:], is_transpose=True,
+                    start=False, stop=(t == PACK - 1),
+                )
+            v_il = sb.tile([P, P, PACK], BF16, name=f"v_il{j}", align_bytes=64)
+            nc.vector.tensor_tensor(
+                v_il[:], vt[:].rearrange("p t e -> p e t"), vsc_t[:].unsqueeze(1).to_broadcast([P, P, PACK]), ALU.mult
+            )
+            codes = sb.tile([P, P], U32, name=f"v_codes{j}", align_bytes=64)
+            scales = sb.tile([P, P], U8, name=f"v_scales{j}", align_bytes=64)
+            nc.vector.quantize_mx(codes[:].bitcast(FP8X4), scales[:], v_il[:].rearrange("p e t -> p (e t)"))
+            return codes, scales
+
+        def weights(h):
+            p_up = sb.tile([P, I], F32, name=f"p_up{h}")
+            p_dn = sb.tile([P, I], F32, name=f"p_dn{h}", tag=("v_win1" if h == 0 else "p_dn1"))
+            sums = sb.tile([P, 2], F32, name=f"psum{h}")
+            flat = s[h][:].rearrange("q t s -> q (t s)")
+            nc.scalar.activation(p_dn[:], flat, ACT.Exp, bias=smin[h][:], scale=-1.0, accum_out=sums[:, 1:2])
+            nc.scalar.activation(p_up[:], flat, ACT.Exp, bias=nsmax[h][:], scale=1.0, accum_out=sums[:, 0:1])
+            rec = sb.tile([P, 2], F32, name=f"rec{h}")
+            nc.vector.reciprocal(rec[:], sums[:])
+            r_up = sb.tile([P, I], F32, name=f"r_up{h}")
+            r_dn = sb.tile([P, I], F32, name=f"r_dn{h}")
+            nc.vector.tensor_scalar(r_dn[:], p_dn[:], rec[:, 1:2], navr[:, h : h + 1], ALU.mult, ALU.mult)
+            nc.vector.tensor_scalar(r_up[:], p_up[:], rec[:, 0:1], None, ALU.mult)
+            wt = bank(f"a{h}", [P, PACK, P], f"wt{h}")
+            for k, r in enumerate((r_dn, r_up)):
+                for t in range(PACK):
+                    nc.tensor.matmul(
+                        wt[:, t, :], lhsT=r[:, t * P : (t + 1) * P], rhs=ident[:], is_transpose=True,
+                        start=(k == 0 and t == 0), stop=(k == 1 and t == PACK - 1),
+                    )
+            w_il = sb.tile([P, P, PACK], BF16, name=f"w_il{h}", align_bytes=64)
+            nc.vector.tensor_tensor(
+                w_il[:], wt[:].rearrange("p t q -> p q t"), wfac_t[:].unsqueeze(1).to_broadcast([P, P, PACK]), ALU.mult
+            )
+            codes = sb.tile([P, P], U32, name=f"w_codes{h}", align_bytes=64)
+            scales = sb.tile([P, P], U8, name=f"w_scales{h}", align_bytes=64)
+            nc.vector.quantize_mx(codes[:].bitcast(FP8X4), scales[:], w_il[:].rearrange("p q t -> p (q t)"))
+            return codes, scales
+
+        vq = [values(0), values(1)]
+        wq = [weights(0), weights(1)]
+        vq.append(values(2))
+        vq.append(values(3))
+
+        o_codes = sb.tile([P, Q], U32, name="o_codes", align_bytes=64)
+        o_scales = sb.tile([P, Q], U8, name="o_scales", align_bytes=64)
+        out_rows = out_0.rearrange("(p j) q -> p j q", j=PACK)
+        o_ps = [bank(f"b{h}", [P, PACK, P], f"o_ps{h}") for h in range(2)]
+        o_f = sb.tile([P, PACK, Q], F32, name="o_f")
+        for j in range(PACK):
+            for h in range(2):
+                nc.tensor.matmul_mx(
+                    o_ps[h][:, j, :], lhsT=vq[j][0][:].bitcast(FP8X4), lhsT_scale=vq[j][1][:],
+                    rhs=wq[h][0][:].bitcast(FP8X4), rhs_scale=wq[h][1][:], start=True, stop=True,
+                )
+            if j == PACK - 2:
+                for h in range(2):
+                    nc.scalar.copy(o_f[:, 0 : PACK - 1, h * P : (h + 1) * P], o_ps[h][:, 0 : PACK - 1, :])
+                nc.sync.dma_start(out_rows[:, 0 : PACK - 1, :], o_f[:, 0 : PACK - 1, :])
+        o_il = [sb.tile([P, P, PACK], BF16, name=f"o_il{h}", align_bytes=64) for h in range(2)]
+        nc.vector.tensor_copy(o_il[1][:], o_ps[1][:].rearrange("p j q -> p q j"))
+        nc.scalar.copy(o_il[0][:], o_ps[0][:].rearrange("p j q -> p q j"))
+        for h in range(2):
+            nc.scalar.copy(o_f[:, PACK - 1, h * P : (h + 1) * P], o_ps[h][:, PACK - 1, :])
+        for h in (1, 0):
+            cols = slice(h * P, (h + 1) * P)
+            nc.vector.quantize_mx(o_codes[:, cols].bitcast(FP8X4), o_scales[:, cols], o_il[h][:].rearrange("p q j -> p (q j)"))
+        nc.sync.dma_start(out_rows[:, PACK - 1, :], o_f[:, PACK - 1, :])
+        nc.sync.dma_start(out_1[0].rearrange("p q r -> p (q r)").bitcast(I32), o_codes[:].bitcast(I32))
+        for quad in range(4):
+            eng = nc.sync if quad % 2 == 0 else nc.scalar
+            eng.dma_start(out_2[0, 4 * quad : 4 * quad + 4, :].bitcast(I32), o_scales[32 * quad : 32 * quad + 4, :].bitcast(I32))

@@ -30,6 +30,7 @@ def tile_attend_interval_twoside_centredvalues_pl_kernel(
     nc = tc.nc
     with ExitStack() as ctx:
         sb = ctx.enter_context(tc.tile_pool(name="sb", bufs=1))
+        vw = ctx.enter_context(tc.tile_pool(name="vw", bufs=1))
         ps = ctx.enter_context(tc.psum_pool(name="ps", bufs=1))
 
         def bank(tag, shape, name):
@@ -37,37 +38,35 @@ def tile_attend_interval_twoside_centredvalues_pl_kernel(
 
         offsets = sb.tile([P, I // 16], U16, name="offsets")
         nc.sync.dma_start(offsets[:], offs)
+        hi_win = sb.tile([P, T], F32, name="hi_win")
+        lo_win = sb.tile([P, T], F32, name="lo_win", tag="lo_win")
+        for win, src in ((hi_win, highend), (lo_win, lowend)):
+            nc.vector.memset(win[0 : P - 1, :].bitcast(I32), 0)
+            nc.sync.dma_start(win[P - 1 : P, :], src[0:1, :])
         kw = sb.tile([P, T], U16, name="kw")
         nc.sync.dma_start(kw[:].bitcast(I32), keys_words[0].bitcast(I32))
         ks = sb.tile([P, T], U8, name="ks")
         for quad in range(4):
             rows = keys_scales[0, 4 * quad : 4 * quad + 4, :].bitcast(I32)
             nc.sync.dma_start(ks[32 * quad : 32 * (quad + 1), :].bitcast(I32), rows.unsqueeze(0).to_broadcast([8, 4, T // 4]))
-        hi_win = sb.tile([P, T], F32, name="hi_win")
-        lo_win = sb.tile([P, T], F32, name="lo_win")
-        for win, src in ((hi_win, highend), (lo_win, lowend)):
-            nc.vector.memset(win[0 : P - 1, :], 0.0)
-            nc.sync.dma_start(win[P - 1 : P, :], src[0:1, :])
         q_raw = sb.tile([P, PACK, Q], F32, name="q_raw")
         nc.sync.dma_start(q_raw[:], query.rearrange("(p j) q -> p j q", j=PACK))
         vals_rows = vals.rearrange("(p j) t -> p j t", j=PACK)
-        v_win = [sb.tile([P, T], F32, name=f"v_win{j}", tag=f"v_win{j}") for j in range(PACK)]
+        v_win = [vw.tile([P, T], F32, name=f"v_win{j}", offset=4 * T * j) for j in range(PACK)]
         lam_t = sb.tile([P, 2], F32, name="lam_t")
         avr_t = sb.tile([P, 2], F32, name="avr_t")
         vsc_t = sb.tile([P, PACK], F32, name="vsc_t")
         wfac_t = sb.tile([P, PACK], F32, name="wfac_t")
-        nc.sync.dma_start(v_win[0][:], vals_rows[:, 0, :])
         with nc.allow_non_contiguous_dma(reason="one value a partition"):
             nc.sync.dma_start(lam_t[:], lam.rearrange("(c p) o -> p (c o)", p=P))
-        nc.sync.dma_start(vsc_t[:], vsc.rearrange("o (p t) -> p (o t)", t=PACK))
-        nc.sync.dma_start(v_win[1][:], vals_rows[:, 1, :])
-        with nc.allow_non_contiguous_dma(reason="one value a partition"):
+            nc.sync.dma_start(v_win[0][:], vals_rows[:, 0, :])
+            nc.sync.dma_start(vsc_t[:], vsc.rearrange("o (p t) -> p (o t)", t=PACK))
             nc.sync.dma_start(avr_t[:], averse.rearrange("(c p) o -> p (c o)", p=P))
-        nc.sync.dma_start(wfac_t[:], wfac.rearrange("o (p t) -> p (o t)", t=PACK))
-        nc.sync.dma_start(v_win[2][:], vals_rows[:, 2, :])
-        nc.sync.dma_start(v_win[3][:], vals_rows[:, 3, :])
+            nc.sync.dma_start(wfac_t[:], wfac.rearrange("o (p t) -> p (o t)", t=PACK))
+        for j in range(1, PACK):
+            nc.sync.dma_start(v_win[j][:], vals_rows[:, j, :])
 
-        ident_bf = sb.tile([P, P], BF16, name="ident_bf")
+        ident_bf = vw.tile([P, P], BF16, name="ident_bf", offset=4 * T * PACK + 4 * I - P)
         make_identity(nc, ident_bf[:])
         ident = sb.tile([P, P], F32, name="ident")
         nc.scalar.activation(ident[:], ident_bf[:], ACT.Copy)
@@ -83,15 +82,15 @@ def tile_attend_interval_twoside_centredvalues_pl_kernel(
             nc.vector.tensor_copy(kg[h][:], kw[:].indirect(half))
             nc.vector.tensor_copy(ksg[h][:], ks[:].indirect(half))
 
-        hi_picked = sb.tile([P, I], F32, name="hi_picked")
-        lo_picked = sb.tile([P, I], F32, name="lo_picked")
+        hi_picked = vw.tile([P, I], F32, name="hi_picked", offset=4 * T * PACK)
+        lo_picked = vw.tile([P, I], F32, name="lo_picked", offset=4 * T * PACK + 4 * I)
         nc.scalar.activation(hi_picked[:], hi_win[:].indirect(offsets[:]), ACT.Copy)
+        nc.scalar.activation(lo_picked[:], lo_win[:].indirect(offsets[:]), ACT.Copy)
         gather_keys(0)
-        nc.vector.tensor_copy(lo_picked[:], lo_win[:].indirect(offsets[:]))
-        nc.scalar.copy(
+        gather_keys(1)
+        nc.vector.tensor_copy(
             q_il[:].rearrange("p (c i) j -> p c j i", i=4), q_raw[:].rearrange("p j (c i) -> p c j i", i=4)
         )
-        gather_keys(1)
         nc.vector.quantize_mx(q_codes[:].bitcast(FP8X4), q_scales[:], q_il[:].rearrange("p q j -> p (q j)"))
 
         ends = []
@@ -99,13 +98,13 @@ def tile_attend_interval_twoside_centredvalues_pl_kernel(
             turned = bank(tag, [P, 4, P], f"turned_{tag}")
             for c in range(4):
                 nc.tensor.transpose(turned[:, c, :], picked[:, c * P : (c + 1) * P], ident[:])
-            col = sb.tile([P, 4], F32, name=f"col_{tag}", tag=f"col_{tag}")
+            col = sb.tile([P, 4], F32, name=f"col_{tag}", tag=("lo_win" if tag == "c2" else "lo_col"))
             nc.scalar.copy(col[:], turned[:, :, P - 1])
             ends.append(col)
         hi_col, lo_col = ends
 
         margin = []
-        for c, tag in enumerate(("a0", "a1", "c0", "c1")):
+        for c, tag in enumerate(("a0", "a1", "b0", "b1")):
             a = bank(tag, [P, Q], f"a{c}")
             cols = slice((c % 2) * P, (c % 2 + 1) * P)
             nc.tensor.matmul_mx(
@@ -118,13 +117,42 @@ def tile_attend_interval_twoside_centredvalues_pl_kernel(
             nc.vector.scalar_tensor_tensor(m[:], a[:], lo_col[:, c : c + 1], up[:], ALU.subtract, ALU.min)
             margin.append(m)
 
+        navr = sb.tile([P, 2], F32, name="navr")
+        nc.gpsimd.tensor_scalar(navr[:], avr_t[:], -1.0, 0.0, ALU.mult, ALU.add)
+
+        def centre_values(j):
+            g = sb.tile([P, I], F32, name=f"g{j}")
+            nc.scalar.activation(g[:], v_win[j][:].indirect(offsets[:]), ACT.Copy)
+            sums = sb.tile([P, I // STRETCH], F32, name=f"vsum{j}")
+            nc.vector.tensor_reduce(sums[:], g[:].rearrange("e (h u) -> e h u", u=STRETCH), AXIS.X, ALU.add)
+            nmean = sb.tile([P, I // STRETCH, 4], F32, name=f"nmean{j}")
+            nc.gpsimd.tensor_scalar(
+                nmean[:], sums[:].unsqueeze(2).to_broadcast([P, I // STRETCH, 4]), -1.0 / STRETCH, 0.0, ALU.mult, ALU.add
+            )
+            vt = bank(f"c{j}", [P, PACK, P], f"vt{j}")
+            for t in range(PACK):
+                nc.tensor.matmul(vt[:, t, :], lhsT=g[:, t::PACK], rhs=ident[:], is_transpose=True, start=(t == 0), stop=False)
+            for t in range(PACK):
+                nc.tensor.matmul(
+                    vt[:, t, :], lhsT=nmean[:].rearrange("e h r -> e (h r)"), rhs=ident[:], is_transpose=True,
+                    start=False, stop=(t == PACK - 1),
+                )
+            return vt
+
+        def quantise_turned(turned, factor, name):
+            il = sb.tile([P, P, PACK], BF16, name=f"{name}_il", align_bytes=64)
+            nc.vector.tensor_tensor(
+                il[:], turned[:].rearrange("p t e -> p e t"), factor[:].unsqueeze(1).to_broadcast([P, P, PACK]), ALU.mult
+            )
+            codes = sb.tile([P, P], U32, name=f"{name}_codes", align_bytes=64)
+            scales = sb.tile([P, P], U8, name=f"{name}_scales", align_bytes=64)
+            nc.vector.quantize_mx(codes[:].bitcast(FP8X4), scales[:], il[:].rearrange("p e t -> p (e t)"))
+            return codes, scales
+
         m_ps = [bank(f"b{h}", [P, I], f"m_ps{h}") for h in range(2)]
         for h in range(2):
             for c in range(4):
                 nc.tensor.transpose(m_ps[h][:, c * P : (c + 1) * P], margin[c][:, h * P : (h + 1) * P], ident[:])
-
-        navr = sb.tile([P, 2], F32, name="navr")
-        nc.gpsimd.tensor_scalar(navr[:], avr_t[:], -1.0, 0.0, ALU.mult, ALU.add)
 
         s = [sb.tile([P, PACK, P], F32, name=f"s{h}") for h in range(2)]
         smin = [sb.tile([P, 1], F32, name=f"smin{h}") for h in range(2)]
@@ -137,60 +165,22 @@ def tile_attend_interval_twoside_centredvalues_pl_kernel(
         for h in range(2):
             nc.vector.tensor_reduce(nsmax[h][:], s[h][:].rearrange("q t s -> q (t s)"), AXIS.X, ALU.max, negate=True)
 
-        def values(j):
-            g = sb.tile([P, I], F32, name=f"g{j}", tag=("col_c2" if j == 0 else f"g{j}"))
-            if j < PACK - 1:
-                nc.scalar.activation(g[:], v_win[j][:].indirect(offsets[:]), ACT.Copy)
-            else:
-                nc.scalar.activation(g[:, 0 : I // 2], v_win[j][:].indirect(offsets[:, 0:16]), ACT.Copy)
-                nc.vector.tensor_copy(g[:, I // 2 : I], v_win[j][:].indirect(offsets[:, 16:32]))
-            if j < PACK - 1:
-                part = g[:].rearrange("e (h u) -> e h u", u=STRETCH)
-                width = STRETCH
-                while width > 1:
-                    width = width // 2
-                    halved = sb.tile([P, I // STRETCH, width], F32, name=f"vpart{j}_{width}")
-                    nc.gpsimd.tensor_tensor(halved[:], part[:, :, 0:width], part[:, :, width : 2 * width], ALU.add)
-                    part = halved[:]
-                total = part
-            else:
-                sums = sb.tile([P, I // STRETCH], F32, name=f"vsum{j}")
-                nc.vector.tensor_reduce(sums[:], g[:].rearrange("e (h u) -> e h u", u=STRETCH), AXIS.X, ALU.add)
-                total = sums[:].unsqueeze(2)
-            nmean = sb.tile([P, I // STRETCH, 4], F32, name=f"nmean{j}")
-            nc.gpsimd.tensor_scalar(
-                nmean[:], total.to_broadcast([P, I // STRETCH, 4]), -1.0 / STRETCH, 0.0, ALU.mult, ALU.add
-            )
-            vt = bank(f"c{j}", [P, PACK, P], f"vt{j}")
-            for t in range(PACK):
-                nc.tensor.matmul(vt[:, t, :], lhsT=g[:, t::PACK], rhs=ident[:], is_transpose=True, start=(t == 0), stop=False)
-            for t in range(PACK):
-                nc.tensor.matmul(
-                    vt[:, t, :], lhsT=nmean[:].rearrange("e h r -> e (h r)"), rhs=ident[:], is_transpose=True,
-                    start=False, stop=(t == PACK - 1),
-                )
-            v_il = sb.tile([P, P, PACK], BF16, name=f"v_il{j}", align_bytes=64)
-            nc.vector.tensor_tensor(
-                v_il[:], vt[:].rearrange("p t e -> p e t"), vsc_t[:].unsqueeze(1).to_broadcast([P, P, PACK]), ALU.mult
-            )
-            codes = sb.tile([P, P], U32, name=f"v_codes{j}", align_bytes=64)
-            scales = sb.tile([P, P], U8, name=f"v_scales{j}", align_bytes=64)
-            nc.vector.quantize_mx(codes[:].bitcast(FP8X4), scales[:], v_il[:].rearrange("p e t -> p (e t)"))
-            return codes, scales
-
-        def weights(h):
-            p_up = sb.tile([P, I], F32, name=f"p_up{h}")
-            p_dn = sb.tile([P, I], F32, name=f"p_dn{h}", tag=("v_win1" if h == 0 else "p_dn1"))
+        def exponentials(h):
+            p_up = vw.tile([P, I], F32, name=f"p_up{h}", offset=4 * T * 2 + 4 * I * (2 + h))
+            p_dn = vw.tile([P, I], F32, name=f"p_dn{h}", offset=4 * T * (1 + h))
             sums = sb.tile([P, 2], F32, name=f"psum{h}")
             flat = s[h][:].rearrange("q t s -> q (t s)")
             nc.scalar.activation(p_dn[:], flat, ACT.Exp, bias=smin[h][:], scale=-1.0, accum_out=sums[:, 1:2])
             nc.scalar.activation(p_up[:], flat, ACT.Exp, bias=nsmax[h][:], scale=1.0, accum_out=sums[:, 0:1])
+            return p_up, p_dn, sums
+
+        def turn_weights(h, p_up, p_dn, sums):
             rec = sb.tile([P, 2], F32, name=f"rec{h}")
             nc.vector.reciprocal(rec[:], sums[:])
-            r_up = sb.tile([P, I], F32, name=f"r_up{h}")
+            r_up = vw.tile([P, I], F32, name=f"r_up{h}", offset=4 * T * 3 + 4 * I * h)
             r_dn = sb.tile([P, I], F32, name=f"r_dn{h}")
             nc.vector.tensor_scalar(r_dn[:], p_dn[:], rec[:, 1:2], navr[:, h : h + 1], ALU.mult, ALU.mult)
-            nc.vector.tensor_scalar(r_up[:], p_up[:], rec[:, 0:1], None, ALU.mult)
+            nc.scalar.activation(r_up[:], p_up[:], ACT.Copy, scale=rec[:, 0:1])
             wt = bank(f"a{h}", [P, PACK, P], f"wt{h}")
             for k, r in enumerate((r_dn, r_up)):
                 for t in range(PACK):
@@ -198,19 +188,17 @@ def tile_attend_interval_twoside_centredvalues_pl_kernel(
                         wt[:, t, :], lhsT=r[:, t * P : (t + 1) * P], rhs=ident[:], is_transpose=True,
                         start=(k == 0 and t == 0), stop=(k == 1 and t == PACK - 1),
                     )
-            w_il = sb.tile([P, P, PACK], BF16, name=f"w_il{h}", align_bytes=64)
-            nc.vector.tensor_tensor(
-                w_il[:], wt[:].rearrange("p t q -> p q t"), wfac_t[:].unsqueeze(1).to_broadcast([P, P, PACK]), ALU.mult
-            )
-            codes = sb.tile([P, P], U32, name=f"w_codes{h}", align_bytes=64)
-            scales = sb.tile([P, P], U8, name=f"w_scales{h}", align_bytes=64)
-            nc.vector.quantize_mx(codes[:].bitcast(FP8X4), scales[:], w_il[:].rearrange("p q t -> p (q t)"))
-            return codes, scales
+            return wt
 
-        vq = [values(0), values(1)]
-        wq = [weights(0), weights(1)]
-        vq.append(values(2))
-        vq.append(values(3))
+        vt = [centre_values(0), centre_values(1)]
+        exps = [exponentials(0), exponentials(1)]
+        wt = [turn_weights(0, *exps[0]), turn_weights(1, *exps[1])]
+        vt.append(centre_values(2))
+        vt.append(centre_values(3))
+        vq = [quantise_turned(vt[0], vsc_t, "v0"), quantise_turned(vt[1], vsc_t, "v1")]
+        wq = [quantise_turned(wt[h], wfac_t, f"w{h}") for h in range(2)]
+        vq.append(quantise_turned(vt[2], vsc_t, "v2"))
+        vq.append(quantise_turned(vt[3], vsc_t, "v3"))
 
         o_codes = sb.tile([P, Q], U32, name="o_codes", align_bytes=64)
         o_scales = sb.tile([P, Q], U8, name="o_scales", align_bytes=64)

@@ -49,20 +49,19 @@ def tile_attend_interval_twoside_centredvalues_pl_kernel(
         for quad in range(4):
             rows = keys_scales[0, 4 * quad : 4 * quad + 4, :].bitcast(I32)
             nc.sync.dma_start(ks[32 * quad : 32 * (quad + 1), :].bitcast(I32), rows.unsqueeze(0).to_broadcast([8, 4, T // 4]))
-        q_raw = sb.tile([P, PACK, Q], F32, name="q_raw")
+        q_raw = sb.tile([P, PACK, Q], F32, name="q_raw", tag="q_raw")
         nc.sync.dma_start(q_raw[:], query.rearrange("(p j) q -> p j q", j=PACK))
         vals_rows = vals.rearrange("(p j) t -> p j t", j=PACK)
         v_win = [vw.tile([P, T], F32, name=f"v_win{j}", offset=4 * T * j) for j in range(PACK)]
-        lam_t = sb.tile([P, 2], F32, name="lam_t")
-        avr_t = sb.tile([P, 2], F32, name="avr_t")
+        row_factors = sb.tile([P, P], F32, name="row_factors")
+        nc.vector.memset(row_factors[0 : P - 4, :], 0.0)
+        nc.sync.dma_start(row_factors[P - 4 : P - 2, :], lam.rearrange("(h q) o -> h (q o)", h=2))
+        nc.sync.dma_start(row_factors[P - 2 : P, :], averse.rearrange("(h q) o -> h (q o)", h=2))
         vsc_t = sb.tile([P, PACK], F32, name="vsc_t")
         wfac_t = sb.tile([P, PACK], F32, name="wfac_t")
-        with nc.allow_non_contiguous_dma(reason="one value a partition"):
-            nc.sync.dma_start(lam_t[:], lam.rearrange("(c p) o -> p (c o)", p=P))
-            nc.sync.dma_start(v_win[0][:], vals_rows[:, 0, :])
-            nc.sync.dma_start(vsc_t[:], vsc.rearrange("o (p t) -> p (o t)", t=PACK))
-            nc.sync.dma_start(avr_t[:], averse.rearrange("(c p) o -> p (c o)", p=P))
-            nc.sync.dma_start(wfac_t[:], wfac.rearrange("o (p t) -> p (o t)", t=PACK))
+        nc.sync.dma_start(v_win[0][:], vals_rows[:, 0, :])
+        nc.sync.dma_start(vsc_t[:], vsc.rearrange("o (p t) -> p (o t)", t=PACK))
+        nc.sync.dma_start(wfac_t[:], wfac.rearrange("o (p t) -> p (o t)", t=PACK))
         for j in range(1, PACK):
             nc.sync.dma_start(v_win[j][:], vals_rows[:, j, :])
 
@@ -88,9 +87,11 @@ def tile_attend_interval_twoside_centredvalues_pl_kernel(
         nc.scalar.activation(lo_picked[:], lo_win[:].indirect(offsets[:]), ACT.Copy)
         gather_keys(0)
         gather_keys(1)
-        nc.vector.tensor_copy(
-            q_il[:].rearrange("p (c i) j -> p c j i", i=4), q_raw[:].rearrange("p j (c i) -> p c j i", i=4)
-        )
+        for copy, cols in ((nc.scalar.copy, slice(0, P)), (nc.vector.tensor_copy, slice(P, Q))):
+            copy(
+                q_il[:, cols, :].rearrange("p (c i) j -> p c j i", i=4),
+                q_raw[:, :, cols].rearrange("p j (c i) -> p c j i", i=4),
+            )
         nc.vector.quantize_mx(q_codes[:].bitcast(FP8X4), q_scales[:], q_il[:].rearrange("p q j -> p (q j)"))
 
         ends = []
@@ -98,10 +99,16 @@ def tile_attend_interval_twoside_centredvalues_pl_kernel(
             turned = bank(tag, [P, 4, P], f"turned_{tag}")
             for c in range(4):
                 nc.tensor.transpose(turned[:, c, :], picked[:, c * P : (c + 1) * P], ident[:])
-            col = sb.tile([P, 4], F32, name=f"col_{tag}", tag=("lo_win" if tag == "c2" else "lo_col"))
+            col = sb.tile([P, 4], F32, name=f"col_{tag}", tag=("lo_win" if tag == "c2" else "q_raw"))
             nc.scalar.copy(col[:], turned[:, :, P - 1])
             ends.append(col)
         hi_col, lo_col = ends
+        factors_ps = bank("c1", [P, P], "factors_ps")
+        nc.tensor.transpose(factors_ps[:], row_factors[:], ident[:])
+        lam_t = sb.tile([P, 2], F32, name="lam_t")
+        navr = sb.tile([P, 2], F32, name="navr")
+        nc.scalar.copy(lam_t[:], factors_ps[:, P - 4 : P - 2])
+        nc.scalar.activation(navr[:], factors_ps[:, P - 2 : P], ACT.Copy, scale=-1.0)
 
         margin = []
         for c, tag in enumerate(("a0", "a1", "b0", "b1")):
@@ -117,9 +124,6 @@ def tile_attend_interval_twoside_centredvalues_pl_kernel(
             nc.vector.scalar_tensor_tensor(m[:], a[:], lo_col[:, c : c + 1], up[:], ALU.subtract, ALU.min)
             margin.append(m)
 
-        navr = sb.tile([P, 2], F32, name="navr")
-        nc.gpsimd.tensor_scalar(navr[:], avr_t[:], -1.0, 0.0, ALU.mult, ALU.add)
-
         def centre_values(j):
             g = sb.tile([P, I], F32, name=f"g{j}")
             nc.scalar.activation(g[:], v_win[j][:].indirect(offsets[:]), ACT.Copy)
@@ -129,7 +133,7 @@ def tile_attend_interval_twoside_centredvalues_pl_kernel(
             nc.gpsimd.tensor_scalar(
                 nmean[:], sums[:].unsqueeze(2).to_broadcast([P, I // STRETCH, 4]), -1.0 / STRETCH, 0.0, ALU.mult, ALU.add
             )
-            vt = bank(f"c{j}", [P, PACK, P], f"vt{j}")
+            vt = bank(("b0", "c1", "c2", "c3")[j], [P, PACK, P], f"vt{j}")
             for t in range(PACK):
                 nc.tensor.matmul(vt[:, t, :], lhsT=g[:, t::PACK], rhs=ident[:], is_transpose=True, start=(t == 0), stop=False)
             for t in range(PACK):
@@ -154,56 +158,64 @@ def tile_attend_interval_twoside_centredvalues_pl_kernel(
             for c in range(4):
                 nc.tensor.transpose(m_ps[h][:, c * P : (c + 1) * P], margin[c][:, h * P : (h + 1) * P], ident[:])
 
-        s = [sb.tile([P, PACK, P], F32, name=f"s{h}") for h in range(2)]
+        s = [sb.tile([P, I], F32, name=f"s{h}") for h in range(2)]
         smin = [sb.tile([P, 1], F32, name=f"smin{h}") for h in range(2)]
         nsmax = [sb.tile([P, 1], F32, name=f"nsmax{h}") for h in range(2)]
         for h in range(2):
             nc.vector.tensor_scalar(
-                s[h][:], m_ps[h][:].rearrange("q (s t) -> q t s", t=PACK), lam_t[:, h : h + 1], None, ALU.mult, ALU.min,
+                s[h][:], m_ps[h][:], lam_t[:, h : h + 1], None, ALU.mult, ALU.min,
                 accum_out=smin[h][:],
             )
         for h in range(2):
-            nc.vector.tensor_reduce(nsmax[h][:], s[h][:].rearrange("q t s -> q (t s)"), AXIS.X, ALU.max, negate=True)
+            nc.vector.tensor_reduce(nsmax[h][:], s[h][:], AXIS.X, ALU.max, negate=True)
 
         def exponentials(h):
-            p_up = vw.tile([P, I], F32, name=f"p_up{h}", offset=4 * T * 2 + 4 * I * (2 + h))
-            p_dn = vw.tile([P, I], F32, name=f"p_dn{h}", offset=4 * T * (1 + h))
+            p_up = sb.tile([P, I], F32, name=f"p_up{h}")
+            p_dn = sb.tile([P, I], F32, name=f"p_dn{h}")
             sums = sb.tile([P, 2], F32, name=f"psum{h}")
-            flat = s[h][:].rearrange("q t s -> q (t s)")
+            flat = s[h][:]
             nc.scalar.activation(p_dn[:], flat, ACT.Exp, bias=smin[h][:], scale=-1.0, accum_out=sums[:, 1:2])
             nc.scalar.activation(p_up[:], flat, ACT.Exp, bias=nsmax[h][:], scale=1.0, accum_out=sums[:, 0:1])
             return p_up, p_dn, sums
 
-        def turn_weights(h, p_up, p_dn, sums):
+        wfac_ps = bank("a0", [P, PACK, P], "wfac_ps")
+        for t in range(PACK):
+            nc.tensor.transpose(wfac_ps[:, t, :], wfac_t[:, t : t + 1].to_broadcast([P, P]), ident[:])
+
+        def weights(h, p_up, p_dn, sums):
             rec = sb.tile([P, 2], F32, name=f"rec{h}")
             nc.vector.reciprocal(rec[:], sums[:])
-            r_up = vw.tile([P, I], F32, name=f"r_up{h}", offset=4 * T * 3 + 4 * I * h)
-            r_dn = sb.tile([P, I], F32, name=f"r_dn{h}")
-            nc.vector.tensor_scalar(r_dn[:], p_dn[:], rec[:, 1:2], navr[:, h : h + 1], ALU.mult, ALU.mult)
-            nc.scalar.activation(r_up[:], p_up[:], ACT.Copy, scale=rec[:, 0:1])
-            wt = bank(f"a{h}", [P, PACK, P], f"wt{h}")
-            for k, r in enumerate((r_dn, r_up)):
-                for t in range(PACK):
-                    nc.tensor.matmul(
-                        wt[:, t, :], lhsT=r[:, t * P : (t + 1) * P], rhs=ident[:], is_transpose=True,
-                        start=(k == 0 and t == 0), stop=(k == 1 and t == PACK - 1),
-                    )
-            return wt
+            ratio = sb.tile([P, 1], F32, name=f"ratio{h}")
+            nc.vector.tensor_scalar(ratio[:], rec[:, 1:2], sums[:, 0:1], navr[:, h : h + 1], ALU.mult, ALU.mult)
+            mix = sb.tile([P, I], F32, name=f"mix{h}")
+            nc.vector.scalar_tensor_tensor(mix[:], p_dn[:], ratio[:], p_up[:], ALU.mult, ALU.add)
+            w_bf = sb.tile([P, P, PACK], BF16, name=f"w_bf{h}")
+            nc.vector.scalar_tensor_tensor(
+                w_bf[:], mix[:].rearrange("q (p t) -> q p t", t=PACK), rec[:, 0:1], wfac_ps[:].rearrange("q t p -> q p t"),
+                ALU.mult, ALU.mult,
+            )
+            words = w_bf[:].rearrange("q p t -> q (p t)").bitcast(F32)
+            wt = bank("a1", [P, 2, P], f"wt{h}")
+            for u in range(2):
+                nc.tensor.transpose(wt[:, u, :], words[:, u::2], ident[:])
+            il = sb.tile([P, P * PACK], BF16, name=f"w_il{h}", align_bytes=64)
+            nc.scalar.copy(il[:].bitcast(F32).rearrange("p (q u) -> p q u", u=2), wt[:].rearrange("p u q -> p q u"))
+            codes = sb.tile([P, P], U32, name=f"w_codes{h}", align_bytes=64)
+            scales = sb.tile([P, P], U8, name=f"w_scales{h}", align_bytes=64)
+            nc.vector.quantize_mx(codes[:].bitcast(FP8X4), scales[:], il[:])
+            return codes, scales
 
         vt = [centre_values(0), centre_values(1)]
         exps = [exponentials(0), exponentials(1)]
-        wt = [turn_weights(0, *exps[0]), turn_weights(1, *exps[1])]
+        wq = [weights(0, *exps[0]), weights(1, *exps[1])]
         vt.append(centre_values(2))
         vt.append(centre_values(3))
-        vq = [quantise_turned(vt[0], vsc_t, "v0"), quantise_turned(vt[1], vsc_t, "v1")]
-        wq = [quantise_turned(wt[h], wfac_t, f"w{h}") for h in range(2)]
-        vq.append(quantise_turned(vt[2], vsc_t, "v2"))
-        vq.append(quantise_turned(vt[3], vsc_t, "v3"))
+        vq = [quantise_turned(vt[j], vsc_t, f"v{j}") for j in range(PACK)]
 
         o_codes = sb.tile([P, Q], U32, name="o_codes", align_bytes=64)
         o_scales = sb.tile([P, Q], U8, name="o_scales", align_bytes=64)
         out_rows = out_0.rearrange("(p j) q -> p j q", j=PACK)
-        o_ps = [bank(f"b{h}", [P, PACK, P], f"o_ps{h}") for h in range(2)]
+        o_ps = [bank(tag, [P, PACK, P], f"o_ps{h}") for h, tag in enumerate(("c0", "b1"))]
         o_f = sb.tile([P, PACK, Q], F32, name="o_f")
         for j in range(PACK):
             for h in range(2):

from contextlib import ExitStack

import concourse.mybir as mybir
from concourse.masks import make_identity

D, T, I, Q, E = 512, 2048, 512, 256, 512
STRETCH = 16
P = 128
PACK = 4

FLOPS = 2 * D * Q * I + 2 * I * E * Q
BYTES = 4 * D * Q + D * T // 2 + D * T // 32 + 2 * 4 * T + 2 * 4 * Q + 2 * 4 * I + 4 * E * T + 2 * P * I // 16 + 5 * E * Q + E * Q // 32

F32 = mybir.dt.float32
BF16 = mybir.dt.bfloat16
I32 = mybir.dt.int32
U32 = mybir.dt.uint32
U16 = mybir.dt.uint16
U8 = mybir.dt.uint8
FP8X4 = mybir.dt.float8_e4m3fn_x4
FP4X4 = mybir.dt.float4_e2m1fn_x4
ALU = mybir.AluOpType
ACT = mybir.ActivationFunctionType
AXIS = mybir.AxisListType


def tile_attend_interval_twoside_centredvalues_pl_kernel(
    tc, query, keys_words, keys_scales, lowend, highend, lam, averse, wfac, vals, vsc, offs, out_0, out_1, out_2
):
    nc = tc.nc
    with ExitStack() as ctx:
        sb = ctx.enter_context(tc.tile_pool(name="sb", bufs=1))
        vw = ctx.enter_context(tc.tile_pool(name="vw", bufs=1))
        ps = ctx.enter_context(tc.psum_pool(name="ps", bufs=1))

        def bank(tag, shape, name):
            return ps.tile(shape, F32, name=name, tag=tag)

        offsets = sb.tile([P, I // 16], U16, name="offsets")
        nc.sync.dma_start(offsets[:], offs)
        hi_win = sb.tile([P, T], F32, name="hi_win")
        lo_win = sb.tile([P, T], F32, name="lo_win", tag="lo_win")
        for win, src in ((hi_win, highend), (lo_win, lowend)):
            nc.vector.memset(win[0 : P - 1, :].bitcast(I32), 0)
            nc.sync.dma_start(win[P - 1 : P, :], src[0:1, :])
        kw = sb.tile([P, T], U16, name="kw")
        nc.sync.dma_start(kw[:].bitcast(I32), keys_words[0].bitcast(I32))
        ks = sb.tile([P, T], U8, name="ks")
        for quad in range(4):
            rows = keys_scales[0, 4 * quad : 4 * quad + 4, :].bitcast(I32)
            nc.sync.dma_start(ks[32 * quad : 32 * (quad + 1), :].bitcast(I32), rows.unsqueeze(0).to_broadcast([8, 4, T // 4]))
        q_raw = sb.tile([P, PACK, Q], F32, name="q_raw", tag="q_raw")
        nc.sync.dma_start(q_raw[:], query.rearrange("(p j) q -> p j q", j=PACK))
        vals_rows = vals.rearrange("(p j) t -> p j t", j=PACK)
        v_win = [vw.tile([P, T], F32, name=f"v_win{j}", offset=4 * T * j) for j in range(PACK)]
        row_factors = sb.tile([P, P], F32, name="row_factors")
        nc.vector.memset(row_factors[0 : P - 4, :], 0.0)
        nc.sync.dma_start(row_factors[P - 4 : P - 2, :], lam.rearrange("(h q) o -> h (q o)", h=2))
        nc.sync.dma_start(row_factors[P - 2 : P, :], averse.rearrange("(h q) o -> h (q o)", h=2))
        vsc_t = sb.tile([P, PACK], F32, name="vsc_t")
        wfac_t = sb.tile([P, PACK], F32, name="wfac_t")
        nc.sync.dma_start(v_win[0][:], vals_rows[:, 0, :])
        nc.sync.dma_start(vsc_t[:], vsc.rearrange("o (p t) -> p (o t)", t=PACK))
        nc.sync.dma_start(wfac_t[:], wfac.rearrange("o (p t) -> p (o t)", t=PACK))
        for j in range(1, PACK):
            nc.sync.dma_start(v_win[j][:], vals_rows[:, j, :])

        ident_bf = vw.tile([P, P], BF16, name="ident_bf", offset=4 * T * PACK + 4 * I - P)
        make_identity(nc, ident_bf[:])
        ident = sb.tile([P, P], F32, name="ident")
        nc.scalar.activation(ident[:], ident_bf[:], ACT.Copy)

        kg = [sb.tile([P, I // 2], U16, name=f"kg{h}", align_bytes=64) for h in range(2)]
        ksg = [sb.tile([P, I // 2], U8, name=f"ksg{h}", align_bytes=64) for h in range(2)]
        q_il = sb.tile([P, Q, PACK], BF16, name="q_il", align_bytes=64)
        q_codes = sb.tile([P, Q], U32, name="q_codes", align_bytes=64)
        q_scales = sb.tile([P, Q], U8, name="q_scales", align_bytes=64)

        def gather_keys(h):
            half = offsets[:, 16 * h : 16 * (h + 1)]
            nc.vector.tensor_copy(kg[h][:], kw[:].indirect(half))
            nc.vector.tensor_copy(ksg[h][:], ks[:].indirect(half))

        hi_picked = vw.tile([P, I], F32, name="hi_picked", offset=4 * T * PACK)
        lo_picked = vw.tile([P, I], F32, name="lo_picked", offset=4 * T * PACK + 4 * I)
        nc.scalar.activation(hi_picked[:], hi_win[:].indirect(offsets[:]), ACT.Copy)
        nc.scalar.activation(lo_picked[:], lo_win[:].indirect(offsets[:]), ACT.Copy)
        gather_keys(0)
        gather_keys(1)
        for copy, cols in ((nc.scalar.copy, slice(0, P)), (nc.vector.tensor_copy, slice(P, Q))):
            copy(
                q_il[:, cols, :].rearrange("p (c i) j -> p c j i", i=4),
                q_raw[:, :, cols].rearrange("p j (c i) -> p c j i", i=4),
            )
        nc.vector.quantize_mx(q_codes[:].bitcast(FP8X4), q_scales[:], q_il[:].rearrange("p q j -> p (q j)"))

        ends = []
        for picked, tag in ((hi_picked, "c2"), (lo_picked, "c3")):
            turned = bank(tag, [P, 4, P], f"turned_{tag}")
            for c in range(4):
                nc.tensor.transpose(turned[:, c, :], picked[:, c * P : (c + 1) * P], ident[:])
            col = sb.tile([P, 4], F32, name=f"col_{tag}", tag=("lo_win" if tag == "c2" else "q_raw"))
            nc.scalar.copy(col[:], turned[:, :, P - 1])
            ends.append(col)
        hi_col, lo_col = ends
        factors_ps = bank("c1", [P, P], "factors_ps")
        nc.tensor.transpose(factors_ps[:], row_factors[:], ident[:])
        lam_t = sb.tile([P, 2], F32, name="lam_t")
        navr = sb.tile([P, 2], F32, name="navr")
        nc.scalar.copy(lam_t[:], factors_ps[:, P - 4 : P - 2])
        nc.scalar.activation(navr[:], factors_ps[:, P - 2 : P], ACT.Copy, scale=-1.0)

        margin = []
        for c, tag in enumerate(("a0", "a1", "b0", "b1")):
            a = bank(tag, [P, Q], f"a{c}")
            cols = slice((c % 2) * P, (c % 2 + 1) * P)
            nc.tensor.matmul_mx(
                a[:], lhsT=kg[c // 2][:, cols].bitcast(FP4X4), lhsT_scale=ksg[c // 2][:, cols],
                rhs=q_codes[:].bitcast(FP8X4), rhs_scale=q_scales[:], start=True, stop=True,
            )
            up = sb.tile([P, Q], F32, name=f"up{c}")
            nc.scalar.activation(up[:], a[:], ACT.Identity, bias=hi_col[:, c : c + 1], scale=-1.0)
            m = sb.tile([P, Q], F32, name=f"m{c}")
            nc.vector.scalar_tensor_tensor(m[:], a[:], lo_col[:, c : c + 1], up[:], ALU.subtract, ALU.min)
            margin.append(m)

        def centre_values(j):
            g = sb.tile([P, I], F32, name=f"g{j}")
            nc.scalar.activation(g[:], v_win[j][:].indirect(offsets[:]), ACT.Copy)
            sums = sb.tile([P, I // STRETCH], F32, name=f"vsum{j}")
            nc.vector.tensor_reduce(sums[:], g[:].rearrange("e (h u) -> e h u", u=STRETCH), AXIS.X, ALU.add)
            nmean = sb.tile([P, I // STRETCH, 4], F32, name=f"nmean{j}")
            nc.gpsimd.tensor_scalar(
                nmean[:], sums[:].unsqueeze(2).to_broadcast([P, I // STRETCH, 4]), -1.0 / STRETCH, 0.0, ALU.mult, ALU.add
            )
            vt = bank(("b0", "c1", "c2", "c3")[j], [P, PACK, P], f"vt{j}")
            for t in range(PACK):
                nc.tensor.matmul(vt[:, t, :], lhsT=g[:, t::PACK], rhs=ident[:], is_transpose=True, start=(t == 0), stop=False)
            for t in range(PACK):
                nc.tensor.matmul(
                    vt[:, t, :], lhsT=nmean[:].rearrange("e h r -> e (h r)"), rhs=ident[:], is_transpose=True,
                    start=False, stop=(t == PACK - 1),
                )
            return vt

        def quantise_turned(turned, factor, name):
            il = sb.tile([P, P, PACK], BF16, name=f"{name}_il", align_bytes=64)
            nc.vector.tensor_tensor(
                il[:], turned[:].rearrange("p t e -> p e t"), factor[:].unsqueeze(1).to_broadcast([P, P, PACK]), ALU.mult
            )
            codes = sb.tile([P, P], U32, name=f"{name}_codes", align_bytes=64)
            scales = sb.tile([P, P], U8, name=f"{name}_scales", align_bytes=64)
            nc.vector.quantize_mx(codes[:].bitcast(FP8X4), scales[:], il[:].rearrange("p e t -> p (e t)"))
            return codes, scales

        m_ps = [bank(f"b{h}", [P, I], f"m_ps{h}") for h in range(2)]
        for h in range(2):
            for c in range(4):
                nc.tensor.transpose(m_ps[h][:, c * P : (c + 1) * P], margin[c][:, h * P : (h + 1) * P], ident[:])

        s = [sb.tile([P, I], F32, name=f"s{h}") for h in range(2)]
        smin = [sb.tile([P, 1], F32, name=f"smin{h}") for h in range(2)]
        nsmax = [sb.tile([P, 1], F32, name=f"nsmax{h}") for h in range(2)]
        for h in range(2):
            nc.vector.tensor_scalar(
                s[h][:], m_ps[h][:], lam_t[:, h : h + 1], None, ALU.mult, ALU.min,
                accum_out=smin[h][:],
            )
        for h in range(2):
            nc.vector.tensor_reduce(nsmax[h][:], s[h][:], AXIS.X, ALU.max, negate=True)

        def exponentials(h):
            p_up = sb.tile([P, I], F32, name=f"p_up{h}")
            p_dn = sb.tile([P, I], F32, name=f"p_dn{h}")
            sums = sb.tile([P, 2], F32, name=f"psum{h}")
            flat = s[h][:]
            nc.scalar.activation(p_dn[:], flat, ACT.Exp, bias=smin[h][:], scale=-1.0, accum_out=sums[:, 1:2])
            nc.scalar.activation(p_up[:], flat, ACT.Exp, bias=nsmax[h][:], scale=1.0, accum_out=sums[:, 0:1])
            return p_up, p_dn, sums

        wfac_ps = bank("a0", [P, PACK, P], "wfac_ps")
        for t in range(PACK):
            nc.tensor.transpose(wfac_ps[:, t, :], wfac_t[:, t : t + 1].to_broadcast([P, P]), ident[:])

        def weights(h, p_up, p_dn, sums):
            rec = sb.tile([P, 2], F32, name=f"rec{h}")
            nc.vector.reciprocal(rec[:], sums[:])
            ratio = sb.tile([P, 1], F32, name=f"ratio{h}")
            nc.vector.tensor_scalar(ratio[:], rec[:, 1:2], sums[:, 0:1], navr[:, h : h + 1], ALU.mult, ALU.mult)
            mix = sb.tile([P, I], F32, name=f"mix{h}")
            nc.vector.scalar_tensor_tensor(mix[:], p_dn[:], ratio[:], p_up[:], ALU.mult, ALU.add)
            w_bf = sb.tile([P, P, PACK], BF16, name=f"w_bf{h}")
            nc.vector.scalar_tensor_tensor(
                w_bf[:], mix[:].rearrange("q (p t) -> q p t", t=PACK), rec[:, 0:1], wfac_ps[:].rearrange("q t p -> q p t"),
                ALU.mult, ALU.mult,
            )
            words = w_bf[:].rearrange("q p t -> q (p t)").bitcast(F32)
            wt = bank("a1", [P, 2, P], f"wt{h}")
            for u in range(2):
                nc.tensor.transpose(wt[:, u, :], words[:, u::2], ident[:])
            il = sb.tile([P, P * PACK], BF16, name=f"w_il{h}", align_bytes=64)
            nc.scalar.copy(il[:].bitcast(F32).rearrange("p (q u) -> p q u", u=2), wt[:].rearrange("p u q -> p q u"))
            codes = sb.tile([P, P], U32, name=f"w_codes{h}", align_bytes=64)
            scales = sb.tile([P, P], U8, name=f"w_scales{h}", align_bytes=64)
            nc.vector.quantize_mx(codes[:].bitcast(FP8X4), scales[:], il[:])
            return codes, scales

        vt = [centre_values(0), centre_values(1)]
        exps = [exponentials(0), exponentials(1)]
        wq = [weights(0, *exps[0]), weights(1, *exps[1])]
        vt.append(centre_values(2))
        vt.append(centre_values(3))
        vq = [quantise_turned(vt[j], vsc_t, f"v{j}") for j in range(PACK)]

        o_codes = sb.tile([P, Q], U32, name="o_codes", align_bytes=64)
        o_scales = sb.tile([P, Q], U8, name="o_scales", align_bytes=64)
        out_rows = out_0.rearrange("(p j) q -> p j q", j=PACK)
        o_ps = [bank(tag, [P, PACK, P], f"o_ps{h}") for h, tag in enumerate(("c0", "b1"))]
        o_f = sb.tile([P, PACK, Q], F32, name="o_f")
        for j in range(PACK):
            for h in range(2):
                nc.tensor.matmul_mx(
                    o_ps[h][:, j, :], lhsT=vq[j][0][:].bitcast(FP8X4), lhsT_scale=vq[j][1][:],
                    rhs=wq[h][0][:].bitcast(FP8X4), rhs_scale=wq[h][1][:], start=True, stop=True,
                )
            if j == PACK - 2:
                for h in range(2):
                    nc.scalar.copy(o_f[:, 0 : PACK - 1, h * P : (h + 1) * P], o_ps[h][:, 0 : PACK - 1, :])
                nc.sync.dma_start(out_rows[:, 0 : PACK - 1, :], o_f[:, 0 : PACK - 1, :])
        o_il = [sb.tile([P, P, PACK], BF16, name=f"o_il{h}", align_bytes=64) for h in range(2)]
        nc.vector.tensor_copy(o_il[1][:], o_ps[1][:].rearrange("p j q -> p q j"))
        nc.scalar.copy(o_il[0][:], o_ps[0][:].rearrange("p j q -> p q j"))
        for h in range(2):
            nc.scalar.copy(o_f[:, PACK - 1, h * P : (h + 1) * P], o_ps[h][:, PACK - 1, :])
        for h in (1, 0):
            cols = slice(h * P, (h + 1) * P)
            nc.vector.quantize_mx(o_codes[:, cols].bitcast(FP8X4), o_scales[:, cols], o_il[h][:].rearrange("p q j -> p (q j)"))
        nc.sync.dma_start(out_rows[:, PACK - 1, :], o_f[:, PACK - 1, :])
        nc.sync.dma_start(out_1[0].rearrange("p q r -> p (q r)").bitcast(I32), o_codes[:].bitcast(I32))
        for quad in range(4):
            eng = nc.sync if quad % 2 == 0 else nc.scalar
            eng.dma_start(out_2[0, 4 * quad : 4 * quad + 4, :].bitcast(I32), o_scales[32 * quad : 32 * quad + 4, :].bitcast(I32))
